import numpy as np
import ml_dtypes


def mxq(x, axis, fmt="e4m3"):
    dtype, down = {"e4m3": (ml_dtypes.float8_e4m3fn, 7), "e5m2": (ml_dtypes.float8_e5m2, 14)}[fmt]
    v = np.moveaxis(np.asarray(x, np.float32).astype(ml_dtypes.bfloat16).astype(np.float64), axis, -1)
    blocks = v.reshape(v.shape[:-1] + (-1, 32))
    amax = np.abs(blocks).max(-1, keepdims=True)
    byte = np.maximum(np.where(amax > 0, np.frexp(amax)[1] - 1 + 127, 0) - down, 1)
    scale = np.exp2(byte - 127.0)
    codes = (blocks / scale).astype(np.float32).astype(dtype).astype(np.float64)
    return np.moveaxis((codes * scale).reshape(v.shape), -1, axis)


WIDE = False


def mx_kscale(k):
    if not WIDE:
        return np.ones(k)
    levels = np.array([10, -10, 5, -5, 0])
    if k % 512:
        return np.exp2(np.random.permutation(np.resize(levels, k // 32))).repeat(32)
    a = np.empty((k // 512, 16))
    for p in range(k // 512):
        a[p, :8] = np.random.permutation(np.resize(levels, 8))
        for g in range(8):
            far = levels[np.abs(levels - a[p, g]) >= 10]
            a[p, g + 8] = far[np.random.randint(len(far))]
    return np.exp2(a.ravel()).repeat(32)


def f64(x):
    return np.asarray(x).astype(np.float64)


def striped(idx):
    return np.tile(idx.reshape(-1, 16).T, (8, 1)).astype(np.uint16)


def unstriped(offs):
    return offs[:16].T.reshape(-1).astype(np.int64)


E2M1 = np.array([0.0, 0.5, 1.0, 1.5, 2.0, 3.0, 4.0, 6.0, -0.0, -0.5, -1.0, -1.5, -2.0, -3.0, -4.0, -6.0])


def pack_weight(w, fmt):
    k, n = w.shape
    w = f64(np.asarray(w, np.float32).astype(ml_dtypes.bfloat16)).reshape(k // 32, 32, n)
    amax = np.abs(w).max(1)
    if fmt == "e4m3":
        byte = np.frexp(amax)[1] - 1 + 127 - 7
    else:
        mant, ex = np.frexp(amax / 6.0)
        byte = np.where(mant > 0.5, ex, ex - 1) + 127
    byte = np.clip(np.where(amax > 0, byte, 1), 1, 254)
    scaled = (w * np.exp2(127.0 - byte)[:, None, :]).reshape(k, n).astype(np.float32)
    by_word = np.ascontiguousarray(scaled.reshape(k // 512, 128, 4, n).transpose(0, 1, 3, 2))
    if fmt == "e4m3":
        words = by_word.astype(ml_dtypes.float8_e4m3fn).view(np.uint8)
    else:
        c = by_word.astype(ml_dtypes.float4_e2m1fn).view(np.uint8) & 0xF
        words = (c[..., 0::2] | (c[..., 1::2] << 4)).reshape(k // 512, 128, 2 * n)
    return np.ascontiguousarray(words), np.ascontiguousarray(byte.astype(np.uint8).reshape(k // 512, 16, n))


def unpack_weight(words, scales, fmt):
    g, _, n = scales.shape
    words = np.ascontiguousarray(words).reshape(g, 128, n, -1)
    if fmt == "e4m3":
        vals = words.view(ml_dtypes.float8_e4m3fn).astype(np.float64)
    else:
        nib = np.empty((g, 128, n, 4), np.uint8)
        nib[..., 0::2] = words & 0xF
        nib[..., 1::2] = words >> 4
        vals = E2M1[nib]
    vals = vals * np.repeat(np.exp2(scales.astype(np.float64) - 127.0), 8, axis=1)[..., None]
    return vals.transpose(0, 1, 3, 2).reshape(g * 512, n)


def relu2(v):
    return np.maximum(v, 0.0) ** 2


K, T, E, C, N = 512, 768, 8, 128, 128
TOP = 4
PAD = 64


def by_expert(wq, xq):
    return np.concatenate([wq[e].T @ xq[:, e * C:(e + 1) * C] for e in range(E)], axis=1)


def setup_inputs():
    n = np.random.standard_normal
    s = mx_kscale(K)[:, None]
    slot_token = np.empty(E * C, np.int64); pos = np.tile(E * C + np.arange(T) % PAD, (TOP, 1)); taken = np.zeros(T, np.int64)
    liked = np.random.randn(T)
    for e in np.random.permutation(E):
        free = np.flatnonzero(taken < TOP); pick = np.random.permutation(free[np.argsort(-(liked[free] + np.random.gumbel(size=free.size)))[:C]]); slot_token[e * C:(e + 1) * C] = pick
        pos[taken[pick], pick] = e * C + np.arange(C); taken[pick] += 1
    g = np.random.uniform(0.2, 0.8, (TOP, T))
    w = [pack_weight(m, "e2m1") for m in n((E, K, N)) / np.sqrt(K) / s[None]]
    return {
        "xT": (n((K, T)) * s).astype(np.float32),
        "w_words": np.stack([m[0] for m in w]),
        "w_scales": np.stack([m[1] for m in w]),
        "b": (0.3 * n((N, E))).astype(np.float32),
        "gate": np.stack([np.tile(r, (N, 1)) for r in g]).astype(np.float32),
        "offs": striped(slot_token),
        "pos1": striped(pos[0]),
        "pos2": striped(pos[1]),
        "pos3": striped(pos[2]),
        "pos4": striped(pos[3]),
    }


def reference(xT, w_words, w_scales, b, gate, offs, pos1, pos2, pos3, pos4):
    idx = unstriped(offs)
    w = np.stack([unpack_weight(w_words[e], w_scales[e], "e2m1") for e in range(E)])
    xq = mxq(f64(xT)[:, idx], 0, "e4m3")
    y = by_expert(w, xq)
    y = relu2(y + np.repeat(f64(b), C, axis=1))
    y = np.concatenate([y, np.zeros((N, PAD))], axis=1)
    return sum(f64(gate[r]) * y[:, unstriped(p)] for r, p in enumerate((pos1, pos2, pos3, pos4)))

@@ -1,0 +1,166 @@
+from contextlib import ExitStack
+
+import concourse.mybir as mybir
+from concourse.masks import make_identity
+
+K, T, E, C, N = 512, 768, 8, 128, 128
+TOP = 4
+PAD = 64
+SLOTS = E * C
+FLOPS = 2 * K * N * SLOTS
+
+F32 = mybir.dt.float32
+BF16 = mybir.dt.bfloat16
+I32 = mybir.dt.int32
+U32 = mybir.dt.uint32
+U16 = mybir.dt.uint16
+U8 = mybir.dt.uint8
+FP8X4 = mybir.dt.float8_e4m3fn_x4
+FP4X4 = mybir.dt.float4_e2m1fn_x4
+ACT = mybir.ActivationFunctionType
+ALU = mybir.AluOpType
+
+P = 128
+PACK = 4
+TOKEN_CHUNKS = ((384, 256), (256, 176), (128, 88))
+SLOT_PIECES = (256, 256, 256, 128, 128)
+SCALAR_SQUARES = 3
+TURNED_CHUNKS = (384, 256)
+
+
+def starts(widths):
+    return [sum(widths[:i]) for i in range(len(widths))]
+
+
+def tile_moe_ecr_lin_relu2_kernel(tc, xT, w_words, w_scales, b, gate, offs, pos1, pos2, pos3, pos4, out):
+    nc = tc.nc
+    with ExitStack() as ctx:
+        lists = ctx.enter_context(tc.tile_pool(name="lists", bufs=1))
+        keep = ctx.enter_context(tc.tile_pool(name="keep", bufs=1))
+        psum = ctx.enter_context(tc.psum_pool(name="psum", bufs=1))
+
+        offs_sb = lists.tile([P, SLOTS // 16], U16, name="offs_sb")
+        pos_sb = [lists.tile([P, T // 16], U16, name=f"pos_sb{r}") for r in range(TOP)]
+
+        x_rows = xT.rearrange("(p j) t -> p j t", j=PACK)
+        raw = []
+        for i, (t0, (width, by_vector)) in enumerate(zip(starts([c[0] for c in TOKEN_CHUNKS]), TOKEN_CHUNKS)):
+            chunk = keep.tile([P, PACK, width], F32, name=f"raw{i}")
+            nc.sync.dma_start(out=chunk[:], in_=x_rows[:, :, t0 : t0 + width])
+            raw.append(chunk)
+        nc.sync.dma_start(offs_sb[:], offs)
+
+        w_codes = keep.tile([P, E, 2 * N], U8, name="w_codes", align_bytes=64)
+        nc.sync.dma_start(out=w_codes[:].bitcast(I32), in_=w_words.rearrange("e a p n -> p (e a) n").bitcast(I32))
+        w_plane = keep.tile([P, E, N], U8, name="w_plane", align_bytes=64)
+        nc.gpsimd.memset(w_plane[:].bitcast(I32), 0)
+        scale_rows = w_scales.rearrange("e a (q r) n -> r q (e a) n", r=4)
+        for r in range(4):
+            nc.sync.dma_start(out=w_plane[r:P:32, :, :].bitcast(I32), in_=scale_rows[r].bitcast(I32))
+        bias = keep.tile([P, E], F32, name="bias")
+        nc.sync.dma_start(out=bias[:], in_=b)
+        for r, pos in enumerate((pos1, pos2, pos3, pos4)):
+            nc.sync.dma_start(pos_sb[r][:], pos)
+
+        x_plane = keep.tile([P, T], U8, name="x_plane", align_bytes=64)
+        nc.gpsimd.memset(x_plane[:], 0)
+        zeros = keep.tile([P, PAD], F32, name="zeros")
+        nc.gpsimd.memset(zeros[:], 0.0)
+        y = keep.tile([P, SLOTS + PAD], F32, name="y")
+        nc.scalar.activation(y[:, SLOTS:], zeros[:], ACT.Relu)
+        ident = keep.tile([P, P], F32, name="ident")
+        make_identity(nc, ident[:])
+
+        turned = sum(TURNED_CHUNKS)
+        gate_rows = keep.tile([P, turned], F32, name="gate_rows")
+        nc.gpsimd.memset(gate_rows[:], 0.0)
+        nc.sync.dma_start(out=gate_rows[0:TOP, :], in_=gate[:, 0, 0:turned])
+        gate_tail = keep.tile([P, TOP, T - turned], F32, name="gate_tail")
+        nc.sync.dma_start(out=gate_tail[:], in_=gate[:, :, turned:].rearrange("r n t -> n r t"))
+        gate_cols = keep.tile([P, turned // P, TOP], F32, name="gate_cols")
+        for b0 in range(0, turned // P, 4):
+            blocks = min(4, turned // P - b0)
+            bank = psum.tile([P, blocks, P], F32, name=f"gate_bank{b0}", tag="work", bufs=3)
+            for k in range(blocks):
+                nc.tensor.transpose(bank[:, k, :], gate_rows[:, (b0 + k) * P : (b0 + k + 1) * P], ident[:])
+            nc.scalar.activation(gate_cols[:, b0 : b0 + blocks, :], bank[:, :, 0:TOP], ACT.Copy)
+
+
+        x_codes = keep.tile([P, T], U32, name="x_codes", align_bytes=64)
+        for i, (t0, (width, by_vector)) in enumerate(zip(starts([c[0] for c in TOKEN_CHUNKS]), TOKEN_CHUNKS)):
+            grouped = keep.tile([P, width, PACK], BF16, name=f"grouped{i}", align_bytes=64)
+            nc.vector.tensor_copy(
+                out=grouped[:, :by_vector, :].rearrange("p (c i) j -> p c j i", i=4),
+                in_=raw[i][:, :, :by_vector].rearrange("p j (c i) -> p c j i", i=4),
+            )
+            nc.scalar.activation(
+                grouped[:, by_vector:, :].rearrange("p (c i) j -> p c j i", i=4),
+                raw[i][:, :, by_vector:].rearrange("p j (c i) -> p c j i", i=4),
+                ACT.Copy,
+            )
+            for q0 in range(0, width, 256):
+                q1 = min(q0 + 256, width)
+                nc.vector.quantize_mx(
+                    out=x_codes[:, t0 + q0 : t0 + q1].bitcast(FP8X4),
+                    scales=x_plane[:, t0 + q0 : t0 + q1],
+                    in_=grouped[:, q0:q1, :].rearrange("p t j -> p (t j)"),
+                )
+
+        for i, (s0, width) in enumerate(zip(starts(SLOT_PIECES), SLOT_PIECES)):
+            picks = offs_sb[:, s0 // 16 : (s0 + width) // 16]
+            slot_codes = keep.tile([P, width], U32, name=f"slot_codes{i}", align_bytes=64)
+            slot_plane = keep.tile([P, width], U8, name=f"slot_plane{i}", align_bytes=64)
+            nc.vector.tensor_copy(slot_codes[:], x_codes[:].indirect(picks))
+            nc.vector.tensor_copy(slot_plane[:], x_plane[:].indirect(picks))
+            sums = psum.tile([P, width], F32, name=f"sums{i}", tag="work", bufs=3)
+            for c0 in range(0, width, C):
+                e = (s0 + c0) // C
+                nc.tensor.matmul_mx(
+                    out=sums[:, c0 : c0 + C],
+                    lhsT=w_codes[:, e, :].bitcast(FP4X4),
+                    lhsT_scale=w_plane[:, e, :],
+                    rhs=slot_codes[:, c0 : c0 + C].bitcast(FP8X4),
+                    rhs_scale=slot_plane[:, c0 : c0 + C],
+                    start=True,
+                    stop=True,
+                )
+            relu = keep.tile([P, width], F32, name=f"relu{i}")
+            for c0 in range(0, width, C):
+                e = (s0 + c0) // C
+                nc.scalar.activation(relu[:, c0 : c0 + C], sums[:, c0 : c0 + C], ACT.Relu, bias=bias[:, e : e + 1])
+            if i < SCALAR_SQUARES:
+                nc.scalar.activation(y[:, s0 : s0 + width], relu[:], ACT.Square)
+            else:
+                nc.vector.tensor_tensor(y[:, s0 : s0 + width], relu[:], relu[:], ALU.mult)
+
+        for i, (t0, width) in enumerate(zip(starts(TURNED_CHUNKS), TURNED_CHUNKS)):
+            blocks = width // P
+            back = [psum.tile([P, P], F32, name=f"back{i}_{k}", tag="back", bufs=5) for k in range(blocks)]
+            for r in range(TOP):
+                picked = keep.tile([P, width], F32, name=f"picked{i}_{r}")
+                nc.vector.tensor_copy(picked[:], y[:].indirect(pos_sb[r][:, t0 // 16 : (t0 + width) // 16]))
+                forth = psum.tile([P, blocks, P], F32, name=f"forth{i}_{r}", tag="work", bufs=3)
+                for k in range(blocks):
+                    nc.tensor.transpose(forth[:, k, :], picked[:, k * P : (k + 1) * P], ident[:])
+                for k in range(blocks):
+                    scaled = keep.tile([P, P], F32, name=f"scaled{i}_{k}_{r}")
+                    nc.scalar.activation(scaled[:], forth[:, k, :], ACT.Copy, scale=gate_cols[:, t0 // P + k, r : r + 1])
+                    nc.tensor.matmul(back[k][:], scaled[:], ident[:], start=(r == 0), stop=(r == TOP - 1), is_transpose=True)
+            result = keep.tile([P, width], F32, name=f"result{i}")
+            for k in range(blocks):
+                nc.scalar.activation(result[:, k * P : (k + 1) * P], back[k][:], ACT.Copy)
+            nc.sync.dma_start(out=out[:, t0 : t0 + width], in_=result[:])
+
+        t0 = sum(TURNED_CHUNKS)
+        width = T - t0
+        products = keep.tile([P, TOP, width], F32, name="products")
+        partial = keep.tile([P, 2, width], F32, name="partial")
+        last = keep.tile([P, width], F32, name="last")
+        for r in range(TOP):
+            picks = pos_sb[r][:, t0 // 16 : T // 16]
+            nc.vector.tensor_tensor(products[:, r, :], y[:].indirect(picks), gate_tail[:, r, :], ALU.mult)
+            if r == 2:
+                nc.vector.tensor_tensor(partial[:, 0, :], products[:, 0, :], products[:, 1, :], ALU.add)
+        nc.vector.tensor_tensor(partial[:, 1, :], partial[:, 0, :], products[:, 2, :], ALU.add)
+        nc.vector.tensor_tensor(last[:], partial[:, 1, :], products[:, 3, :], ALU.add)
+        nc.sync.dma_start(out=out[:, t0:], in_=last[:])

@@ -22,7 +22,7 @@ ALU = mybir.AluOpType
 
 P = 128
 PACK = 4
-TOKEN_CHUNKS = ((384, 256), (256, 176), (128, 88))
+TOKEN_CHUNKS = ((256, 128), (256, 128), (128, 0), (128, 88))
 SLOT_PIECES = (256, 256, 256, 128, 128)
 SCALAR_SQUARES = 3
 TURNED_CHUNKS = (384, 256)
@@ -48,15 +48,15 @@ def tile_moe_ecr_lin_relu2_kernel(tc, xT, w_words, w_scales, b, gate, offs, pos1
             chunk = keep.tile([P, PACK, width], F32, name=f"raw{i}")
             nc.sync.dma_start(out=chunk[:], in_=x_rows[:, :, t0 : t0 + width])
             raw.append(chunk)
+        w_plane = keep.tile([P, E, N], U8, name="w_plane", align_bytes=64)
+        nc.vector.memset(w_plane[:].bitcast(I32), 0)
+        scale_rows = w_scales.rearrange("e a (q r) n -> r q (e a) n", r=4)
+        for r in range(4):
+            nc.sync.dma_start(out=w_plane[r:P:32, :, :].bitcast(I32), in_=scale_rows[r].bitcast(I32))
         nc.sync.dma_start(offs_sb[:], offs)
 
         w_codes = keep.tile([P, E, 2 * N], U8, name="w_codes", align_bytes=64)
         nc.sync.dma_start(out=w_codes[:].bitcast(I32), in_=w_words.rearrange("e a p n -> p (e a) n").bitcast(I32))
-        w_plane = keep.tile([P, E, N], U8, name="w_plane", align_bytes=64)
-        nc.gpsimd.memset(w_plane[:].bitcast(I32), 0)
-        scale_rows = w_scales.rearrange("e a (q r) n -> r q (e a) n", r=4)
-        for r in range(4):
-            nc.sync.dma_start(out=w_plane[r:P:32, :, :].bitcast(I32), in_=scale_rows[r].bitcast(I32))
         bias = keep.tile([P, E], F32, name="bias")
         nc.sync.dma_start(out=bias[:], in_=b)
         for r, pos in enumerate((pos1, pos2, pos3, pos4)):
@@ -71,28 +71,19 @@ def tile_moe_ecr_lin_relu2_kernel(tc, xT, w_words, w_scales, b, gate, offs, pos1
         ident = keep.tile([P, P], F32, name="ident")
         make_identity(nc, ident[:])
 
-        turned = sum(TURNED_CHUNKS)
-        gate_rows = keep.tile([P, turned], F32, name="gate_rows")
-        nc.gpsimd.memset(gate_rows[:], 0.0)
-        nc.sync.dma_start(out=gate_rows[0:TOP, :], in_=gate[:, 0, 0:turned])
-        gate_tail = keep.tile([P, TOP, T - turned], F32, name="gate_tail")
-        nc.sync.dma_start(out=gate_tail[:], in_=gate[:, :, turned:].rearrange("r n t -> n r t"))
-        gate_cols = keep.tile([P, turned // P, TOP], F32, name="gate_cols")
-        for b0 in range(0, turned // P, 4):
-            blocks = min(4, turned // P - b0)
-            bank = psum.tile([P, blocks, P], F32, name=f"gate_bank{b0}", tag="work", bufs=3)
-            for k in range(blocks):
-                nc.tensor.transpose(bank[:, k, :], gate_rows[:, (b0 + k) * P : (b0 + k + 1) * P], ident[:])
-            nc.scalar.activation(gate_cols[:, b0 : b0 + blocks, :], bank[:, :, 0:TOP], ACT.Copy)
+        gate_sb = [keep.tile([P, T], F32, name=f"gate_sb{r}") for r in range(TOP)]
+        for r in range(TOP):
+            nc.sync.dma_start(out=gate_sb[r][:], in_=gate[r])
 
 
         x_codes = keep.tile([P, T], U32, name="x_codes", align_bytes=64)
         for i, (t0, (width, by_vector)) in enumerate(zip(starts([c[0] for c in TOKEN_CHUNKS]), TOKEN_CHUNKS)):
             grouped = keep.tile([P, width, PACK], BF16, name=f"grouped{i}", align_bytes=64)
-            nc.vector.tensor_copy(
-                out=grouped[:, :by_vector, :].rearrange("p (c i) j -> p c j i", i=4),
-                in_=raw[i][:, :, :by_vector].rearrange("p j (c i) -> p c j i", i=4),
-            )
+            if by_vector:
+                nc.vector.tensor_copy(
+                    out=grouped[:, :by_vector, :].rearrange("p (c i) j -> p c j i", i=4),
+                    in_=raw[i][:, :, :by_vector].rearrange("p j (c i) -> p c j i", i=4),
+                )
             nc.scalar.activation(
                 grouped[:, by_vector:, :].rearrange("p (c i) j -> p c j i", i=4),
                 raw[i][:, :, by_vector:].rearrange("p j (c i) -> p c j i", i=4),
@@ -135,20 +126,19 @@ def tile_moe_ecr_lin_relu2_kernel(tc, xT, w_words, w_scales, b, gate, offs, pos1
 
         for i, (t0, width) in enumerate(zip(starts(TURNED_CHUNKS), TURNED_CHUNKS)):
             blocks = width // P
-            back = [psum.tile([P, P], F32, name=f"back{i}_{k}", tag="back", bufs=5) for k in range(blocks)]
+            weighted = [keep.tile([P, width], F32, name=f"weighted{i}_{r}") for r in range(TOP)]
             for r in range(TOP):
-                picked = keep.tile([P, width], F32, name=f"picked{i}_{r}")
-                nc.vector.tensor_copy(picked[:], y[:].indirect(pos_sb[r][:, t0 // 16 : (t0 + width) // 16]))
-                forth = psum.tile([P, blocks, P], F32, name=f"forth{i}_{r}", tag="work", bufs=3)
-                for k in range(blocks):
-                    nc.tensor.transpose(forth[:, k, :], picked[:, k * P : (k + 1) * P], ident[:])
-                for k in range(blocks):
-                    scaled = keep.tile([P, P], F32, name=f"scaled{i}_{k}_{r}")
-                    nc.scalar.activation(scaled[:], forth[:, k, :], ACT.Copy, scale=gate_cols[:, t0 // P + k, r : r + 1])
-                    nc.tensor.matmul(back[k][:], scaled[:], ident[:], start=(r == 0), stop=(r == TOP - 1), is_transpose=True)
+                nc.vector.tensor_tensor(weighted[r][:], y[:].indirect(pos_sb[r][:, t0 // 16 : (t0 + width) // 16]), gate_sb[r][:, t0 : t0 + width], ALU.mult)
             result = keep.tile([P, width], F32, name=f"result{i}")
+            back = psum.tile([P, blocks, P], F32, name=f"back{i}", tag="back", bufs=2)
             for k in range(blocks):
-                nc.scalar.activation(result[:, k * P : (k + 1) * P], back[k][:], ACT.Copy)
+                forth = psum.tile([P, P], F32, name=f"forth{i}_{k}", tag="work", bufs=3)
+                for r in range(TOP):
+                    nc.tensor.matmul(forth[:], weighted[r][:, k * P : (k + 1) * P], ident[:], start=(r == 0), stop=(r == TOP - 1), is_transpose=True)
+                summed = keep.tile([P, P], F32, name=f"summed{i}_{k}")
+                nc.scalar.activation(summed[:], forth[:], ACT.Copy)
+                nc.tensor.transpose(back[:, k, :], summed[:], ident[:])
+            nc.scalar.activation(result[:], back[:].rearrange("p k t -> p (k t)"), ACT.Copy)
             nc.sync.dma_start(out=out[:, t0 : t0 + width], in_=result[:])
 
         t0 = sum(TURNED_CHUNKS)
@@ -158,7 +148,7 @@ def tile_moe_ecr_lin_relu2_kernel(tc, xT, w_words, w_scales, b, gate, offs, pos1
         last = keep.tile([P, width], F32, name="last")
         for r in range(TOP):
             picks = pos_sb[r][:, t0 // 16 : T // 16]
-            nc.vector.tensor_tensor(products[:, r, :], y[:].indirect(picks), gate_tail[:, r, :], ALU.mult)
+            nc.vector.tensor_tensor(products[:, r, :], y[:].indirect(picks), gate_sb[r][:, t0:], ALU.mult)
             if r == 2:
                 nc.vector.tensor_tensor(partial[:, 0, :], products[:, 0, :], products[:, 1, :], ALU.add)
         nc.vector.tensor_tensor(partial[:, 1, :], partial[:, 0, :], products[:, 2, :], ALU.add)

@@ -71,10 +71,15 @@ def tile_moe_ecr_lin_relu2_kernel(tc, xT, w_words, w_scales, b, gate, offs, pos1
         ident = keep.tile([P, P], F32, name="ident")
         make_identity(nc, ident[:])
 
-        gate_sb = [keep.tile([P, T], F32, name=f"gate_sb{r}") for r in range(TOP)]
+        turned = sum(TURNED_CHUNKS)
+        gate_sb = []
         for r in range(TOP):
-            nc.sync.dma_start(out=gate_sb[r][:], in_=gate[r])
-
+            width = T if r == 0 else turned
+            gate_row = keep.tile([P, width], F32, name=f"gate{r}")
+            nc.sync.dma_start(out=gate_row[:], in_=gate[r, :, 0:width])
+            gate_sb.append(gate_row)
+        gate_tail = keep.tile([P, TOP - 1, T - turned], F32, name="gate_tail")
+        nc.sync.dma_start(out=gate_tail[:], in_=gate[1:TOP, :, turned:].rearrange("r n t -> n r t"))
 
         x_codes = keep.tile([P, T], U32, name="x_codes", align_bytes=64)
         for i, (t0, (width, by_vector)) in enumerate(zip(starts([c[0] for c in TOKEN_CHUNKS]), TOKEN_CHUNKS)):
@@ -103,7 +108,7 @@ def tile_moe_ecr_lin_relu2_kernel(tc, xT, w_words, w_scales, b, gate, offs, pos1
             slot_plane = keep.tile([P, width], U8, name=f"slot_plane{i}", align_bytes=64)
             nc.vector.tensor_copy(slot_codes[:], x_codes[:].indirect(picks))
             nc.vector.tensor_copy(slot_plane[:], x_plane[:].indirect(picks))
-            sums = psum.tile([P, width], F32, name=f"sums{i}", tag="work", bufs=3)
+            sums = psum.tile([P, width], F32, name=f"sums{i}", tag="work", bufs=5)
             for c0 in range(0, width, C):
                 e = (s0 + c0) // C
                 nc.tensor.matmul_mx(
@@ -124,33 +129,37 @@ def tile_moe_ecr_lin_relu2_kernel(tc, xT, w_words, w_scales, b, gate, offs, pos1
             else:
                 nc.vector.tensor_tensor(y[:, s0 : s0 + width], relu[:], relu[:], ALU.mult)
 
+        forth = [psum.tile([P, P], F32, name=f"forth{k}", tag="work", bufs=5) for k in range(turned // P)]
+
+        def weigh(r, t0, width, gate_cols):
+            weighted = keep.tile([P, width], F32, name=f"weighted{r}_{t0}")
+            nc.vector.tensor_tensor(weighted[:], y[:].indirect(pos_sb[r][:, t0 // 16 : (t0 + width) // 16]), gate_cols, ALU.mult)
+            return weighted
+
+        def turn_and_add(r, weighted, t0, width):
+            for c0 in range(0, width, P):
+                nc.tensor.matmul(forth[(t0 + c0) // P][:], weighted[:, c0 : c0 + P], ident[:], start=(r == 0), stop=(r == TOP - 1), is_transpose=True)
+
+        first = weigh(0, 0, T, gate_sb[0][:])
+        turn_and_add(0, first, 0, turned)
+        for r in range(1, TOP - 1):
+            turn_and_add(r, weigh(r, 0, turned, gate_sb[r][:]), 0, turned)
         for i, (t0, width) in enumerate(zip(starts(TURNED_CHUNKS), TURNED_CHUNKS)):
-            blocks = width // P
-            weighted = [keep.tile([P, width], F32, name=f"weighted{i}_{r}") for r in range(TOP)]
-            for r in range(TOP):
-                nc.vector.tensor_tensor(weighted[r][:], y[:].indirect(pos_sb[r][:, t0 // 16 : (t0 + width) // 16]), gate_sb[r][:, t0 : t0 + width], ALU.mult)
+            turn_and_add(TOP - 1, weigh(TOP - 1, t0, width, gate_sb[TOP - 1][:, t0 : t0 + width]), t0, width)
+            back = psum.tile([P, width], F32, name=f"back{i}", tag="back", bufs=2)
+            for c0 in range(0, width, P):
+                summed = keep.tile([P, P], F32, name=f"summed{t0 + c0}")
+                nc.scalar.activation(summed[:], forth[(t0 + c0) // P][:], ACT.Copy)
+                nc.tensor.transpose(back[:, c0 : c0 + P], summed[:], ident[:])
             result = keep.tile([P, width], F32, name=f"result{i}")
-            back = psum.tile([P, blocks, P], F32, name=f"back{i}", tag="back", bufs=2)
-            for k in range(blocks):
-                forth = psum.tile([P, P], F32, name=f"forth{i}_{k}", tag="work", bufs=3)
-                for r in range(TOP):
-                    nc.tensor.matmul(forth[:], weighted[r][:, k * P : (k + 1) * P], ident[:], start=(r == 0), stop=(r == TOP - 1), is_transpose=True)
-                summed = keep.tile([P, P], F32, name=f"summed{i}_{k}")
-                nc.scalar.activation(summed[:], forth[:], ACT.Copy)
-                nc.tensor.transpose(back[:, k, :], summed[:], ident[:])
-            nc.scalar.activation(result[:], back[:].rearrange("p k t -> p (k t)"), ACT.Copy)
+            nc.scalar.activation(result[:], back[:], ACT.Copy)
             nc.sync.dma_start(out=out[:, t0 : t0 + width], in_=result[:])
 
-        t0 = sum(TURNED_CHUNKS)
-        width = T - t0
-        products = keep.tile([P, TOP, width], F32, name="products")
-        partial = keep.tile([P, 2, width], F32, name="partial")
-        last = keep.tile([P, width], F32, name="last")
-        for r in range(TOP):
-            picks = pos_sb[r][:, t0 // 16 : T // 16]
-            nc.vector.tensor_tensor(products[:, r, :], y[:].indirect(picks), gate_sb[r][:, t0:], ALU.mult)
-            if r == 2:
-                nc.vector.tensor_tensor(partial[:, 0, :], products[:, 0, :], products[:, 1, :], ALU.add)
-        nc.vector.tensor_tensor(partial[:, 1, :], partial[:, 0, :], products[:, 2, :], ALU.add)
-        nc.vector.tensor_tensor(last[:], partial[:, 1, :], products[:, 3, :], ALU.add)
-        nc.sync.dma_start(out=out[:, t0:], in_=last[:])
+        tail = [weigh(r, turned, T - turned, gate_tail[:, r - 1, :]) for r in (1, 2)]
+        partial = keep.tile([P, 2, T - turned], F32, name="partial")
+        nc.vector.tensor_tensor(partial[:, 0, :], first[:, turned:], tail[0][:], ALU.add)
+        tail.append(weigh(TOP - 1, turned, T - turned, gate_tail[:, TOP - 2, :]))
+        nc.vector.tensor_tensor(partial[:, 1, :], partial[:, 0, :], tail[1][:], ALU.add)
+        last = keep.tile([P, T - turned], F32, name="last")
+        nc.vector.tensor_tensor(last[:], partial[:, 1, :], tail[2][:], ALU.add)
+        nc.sync.dma_start(out=out[:, turned:], in_=last[:])

@@ -22,7 +22,8 @@ ALU = mybir.AluOpType
 
 P = 128
 PACK = 4
-TOKEN_CHUNKS = ((256, 128), (256, 128), (128, 0), (128, 88))
+LOAD_CHUNKS = (256, 256, 128, 128)
+CAST_PIECES = ((256, 128), (256, 128), (128, 0), (128, 88))
 SLOT_PIECES = (256, 256, 256, 128, 128)
 SCALAR_SQUARES = 3
 TURNED_CHUNKS = (384, 256)
@@ -44,10 +45,10 @@ def tile_moe_ecr_lin_relu2_kernel(tc, xT, w_words, w_scales, b, gate, offs, pos1
 
         x_rows = xT.rearrange("(p j) t -> p j t", j=PACK)
         raw = []
-        for i, (t0, (width, by_vector)) in enumerate(zip(starts([c[0] for c in TOKEN_CHUNKS]), TOKEN_CHUNKS)):
-            chunk = keep.tile([P, PACK, width], F32, name=f"raw{i}")
+        for t0, width in zip(starts(LOAD_CHUNKS), LOAD_CHUNKS):
+            chunk = keep.tile([P, PACK, width], F32, name=f"raw{t0}")
             nc.sync.dma_start(out=chunk[:], in_=x_rows[:, :, t0 : t0 + width])
-            raw.append(chunk)
+            raw.append((t0, t0 + width, chunk))
         w_plane = keep.tile([P, E, N], U8, name="w_plane", align_bytes=64)
         nc.vector.memset(w_plane[:].bitcast(I32), 0)
         scale_rows = w_scales.rearrange("e a (q r) n -> r q (e a) n", r=4)
@@ -74,33 +75,32 @@ def tile_moe_ecr_lin_relu2_kernel(tc, xT, w_words, w_scales, b, gate, offs, pos1
         turned = sum(TURNED_CHUNKS)
         gate_sb = []
         for r in range(TOP):
-            width = T if r == 0 else turned
-            gate_row = keep.tile([P, width], F32, name=f"gate{r}")
-            nc.sync.dma_start(out=gate_row[:], in_=gate[r, :, 0:width])
+            gate_row = keep.tile([P, turned], F32, name=f"gate{r}")
+            nc.sync.dma_start(out=gate_row[:], in_=gate[r, :, 0:turned])
             gate_sb.append(gate_row)
-        gate_tail = keep.tile([P, TOP - 1, T - turned], F32, name="gate_tail")
-        nc.sync.dma_start(out=gate_tail[:], in_=gate[1:TOP, :, turned:].rearrange("r n t -> n r t"))
+        gate_tail = keep.tile([P, TOP, T - turned], F32, name="gate_tail")
+        nc.sync.dma_start(out=gate_tail[:], in_=gate[:, :, turned:].rearrange("r n t -> n r t"))
 
         x_codes = keep.tile([P, T], U32, name="x_codes", align_bytes=64)
-        for i, (t0, (width, by_vector)) in enumerate(zip(starts([c[0] for c in TOKEN_CHUNKS]), TOKEN_CHUNKS)):
-            grouped = keep.tile([P, width, PACK], BF16, name=f"grouped{i}", align_bytes=64)
-            if by_vector:
+        for t0, (width, by_vector) in zip(starts([c[0] for c in CAST_PIECES]), CAST_PIECES):
+            source = [chunk[:, :, t0 - lo : t0 - lo + width] for lo, hi, chunk in raw if lo <= t0 < hi][0]
+            grouped = keep.tile([P, width, PACK], BF16, name=f"grouped{t0}", align_bytes=64)
+            if by_vector > 0:
                 nc.vector.tensor_copy(
                     out=grouped[:, :by_vector, :].rearrange("p (c i) j -> p c j i", i=4),
-                    in_=raw[i][:, :, :by_vector].rearrange("p j (c i) -> p c j i", i=4),
+                    in_=source[:, :, :by_vector].rearrange("p j (c i) -> p c j i", i=4),
                 )
-            nc.scalar.activation(
-                grouped[:, by_vector:, :].rearrange("p (c i) j -> p c j i", i=4),
-                raw[i][:, :, by_vector:].rearrange("p j (c i) -> p c j i", i=4),
-                ACT.Copy,
+            if by_vector < width:
+                nc.scalar.activation(
+                    grouped[:, by_vector:, :].rearrange("p (c i) j -> p c j i", i=4),
+                    source[:, :, by_vector:].rearrange("p j (c i) -> p c j i", i=4),
+                    ACT.Copy,
+                )
+            nc.vector.quantize_mx(
+                out=x_codes[:, t0 : t0 + width].bitcast(FP8X4),
+                scales=x_plane[:, t0 : t0 + width],
+                in_=grouped[:].rearrange("p t j -> p (t j)"),
             )
-            for q0 in range(0, width, 256):
-                q1 = min(q0 + 256, width)
-                nc.vector.quantize_mx(
-                    out=x_codes[:, t0 + q0 : t0 + q1].bitcast(FP8X4),
-                    scales=x_plane[:, t0 + q0 : t0 + q1],
-                    in_=grouped[:, q0:q1, :].rearrange("p t j -> p (t j)"),
-                )
 
         for i, (s0, width) in enumerate(zip(starts(SLOT_PIECES), SLOT_PIECES)):
             picks = offs_sb[:, s0 // 16 : (s0 + width) // 16]
@@ -140,9 +140,7 @@ def tile_moe_ecr_lin_relu2_kernel(tc, xT, w_words, w_scales, b, gate, offs, pos1
             for c0 in range(0, width, P):
                 nc.tensor.matmul(forth[(t0 + c0) // P][:], weighted[:, c0 : c0 + P], ident[:], start=(r == 0), stop=(r == TOP - 1), is_transpose=True)
 
-        first = weigh(0, 0, T, gate_sb[0][:])
-        turn_and_add(0, first, 0, turned)
-        for r in range(1, TOP - 1):
+        for r in range(TOP - 1):
             turn_and_add(r, weigh(r, 0, turned, gate_sb[r][:]), 0, turned)
         for i, (t0, width) in enumerate(zip(starts(TURNED_CHUNKS), TURNED_CHUNKS)):
             turn_and_add(TOP - 1, weigh(TOP - 1, t0, width, gate_sb[TOP - 1][:, t0 : t0 + width]), t0, width)
@@ -155,11 +153,11 @@ def tile_moe_ecr_lin_relu2_kernel(tc, xT, w_words, w_scales, b, gate, offs, pos1
             nc.scalar.activation(result[:], back[:], ACT.Copy)
             nc.sync.dma_start(out=out[:, t0 : t0 + width], in_=result[:])
 
-        tail = [weigh(r, turned, T - turned, gate_tail[:, r - 1, :]) for r in (1, 2)]
+        tail = [weigh(r, turned, T - turned, gate_tail[:, r, :]) for r in range(TOP - 1)]
         partial = keep.tile([P, 2, T - turned], F32, name="partial")
-        nc.vector.tensor_tensor(partial[:, 0, :], first[:, turned:], tail[0][:], ALU.add)
-        tail.append(weigh(TOP - 1, turned, T - turned, gate_tail[:, TOP - 2, :]))
-        nc.vector.tensor_tensor(partial[:, 1, :], partial[:, 0, :], tail[1][:], ALU.add)
+        nc.vector.tensor_tensor(partial[:, 0, :], tail[0][:], tail[1][:], ALU.add)
+        tail.append(weigh(TOP - 1, turned, T - turned, gate_tail[:, TOP - 1, :]))
+        nc.vector.tensor_tensor(partial[:, 1, :], partial[:, 0, :], tail[2][:], ALU.add)
         last = keep.tile([P, T - turned], F32, name="last")
-        nc.vector.tensor_tensor(last[:], partial[:, 1, :], tail[2][:], ALU.add)
+        nc.vector.tensor_tensor(last[:], partial[:, 1, :], tail[3][:], ALU.add)
         nc.sync.dma_start(out=out[:, turned:], in_=last[:])

from contextlib import ExitStack

import concourse.mybir as mybir
from concourse.masks import make_identity

K, T, E, C, N = 512, 768, 8, 128, 128
TOP = 4
PAD = 64
SLOTS = E * C
FLOPS = 2 * K * N * SLOTS

F32 = mybir.dt.float32
BF16 = mybir.dt.bfloat16
I32 = mybir.dt.int32
U32 = mybir.dt.uint32
U16 = mybir.dt.uint16
U8 = mybir.dt.uint8
FP8X4 = mybir.dt.float8_e4m3fn_x4
FP4X4 = mybir.dt.float4_e2m1fn_x4
ACT = mybir.ActivationFunctionType
ALU = mybir.AluOpType

P = 128
PACK = 4
LOAD_CHUNKS = (256, 256, 128, 128)
CAST_PIECES = ((256, 128), (256, 128), (128, 0), (128, 88))
SLOT_PIECES = (256, 256, 256, 128, 128)
SCALAR_SQUARES = 3
TURNED_CHUNKS = (384, 256)


def starts(widths):
    return [sum(widths[:i]) for i in range(len(widths))]


def tile_moe_ecr_lin_relu2_kernel(tc, xT, w_words, w_scales, b, gate, offs, pos1, pos2, pos3, pos4, out):
    nc = tc.nc
    with ExitStack() as ctx:
        lists = ctx.enter_context(tc.tile_pool(name="lists", bufs=1))
        keep = ctx.enter_context(tc.tile_pool(name="keep", bufs=1))
        psum = ctx.enter_context(tc.psum_pool(name="psum", bufs=1))

        offs_sb = lists.tile([P, SLOTS // 16], U16, name="offs_sb")
        pos_sb = [lists.tile([P, T // 16], U16, name=f"pos_sb{r}") for r in range(TOP)]

        x_rows = xT.rearrange("(p j) t -> p j t", j=PACK)
        raw = []
        for t0, width in zip(starts(LOAD_CHUNKS), LOAD_CHUNKS):
            chunk = keep.tile([P, PACK, width], F32, name=f"raw{t0}")
            nc.sync.dma_start(out=chunk[:], in_=x_rows[:, :, t0 : t0 + width])
            raw.append((t0, t0 + width, chunk))
        w_plane = keep.tile([P, E, N], U8, name="w_plane", align_bytes=64)
        nc.vector.memset(w_plane[:].bitcast(I32), 0)
        scale_rows = w_scales.rearrange("e a (q r) n -> r q (e a) n", r=4)
        for r in range(4):
            nc.sync.dma_start(out=w_plane[r:P:32, :, :].bitcast(I32), in_=scale_rows[r].bitcast(I32))
        nc.sync.dma_start(offs_sb[:], offs)

        w_codes = keep.tile([P, E, 2 * N], U8, name="w_codes", align_bytes=64)
        nc.sync.dma_start(out=w_codes[:].bitcast(I32), in_=w_words.rearrange("e a p n -> p (e a) n").bitcast(I32))
        bias = keep.tile([P, E], F32, name="bias")
        nc.sync.dma_start(out=bias[:], in_=b)
        for r, pos in enumerate((pos1, pos2, pos3, pos4)):
            nc.sync.dma_start(pos_sb[r][:], pos)

        x_plane = keep.tile([P, T], U8, name="x_plane", align_bytes=64)
        nc.gpsimd.memset(x_plane[:], 0)
        zeros = keep.tile([P, PAD], F32, name="zeros")
        nc.gpsimd.memset(zeros[:], 0.0)
        y = keep.tile([P, SLOTS + PAD], F32, name="y")
        nc.scalar.activation(y[:, SLOTS:], zeros[:], ACT.Relu)
        ident = keep.tile([P, P], F32, name="ident")
        make_identity(nc, ident[:])

        turned = sum(TURNED_CHUNKS)
        gate_sb = []
        for r in range(TOP):
            gate_row = keep.tile([P, turned], F32, name=f"gate{r}")
            nc.sync.dma_start(out=gate_row[:], in_=gate[r, :, 0:turned])
            gate_sb.append(gate_row)
        gate_tail = keep.tile([P, TOP, T - turned], F32, name="gate_tail")
        nc.sync.dma_start(out=gate_tail[:], in_=gate[:, :, turned:].rearrange("r n t -> n r t"))

        x_codes = keep.tile([P, T], U32, name="x_codes", align_bytes=64)
        for t0, (width, by_vector) in zip(starts([c[0] for c in CAST_PIECES]), CAST_PIECES):
            source = [chunk[:, :, t0 - lo : t0 - lo + width] for lo, hi, chunk in raw if lo <= t0 < hi][0]
            grouped = keep.tile([P, width, PACK], BF16, name=f"grouped{t0}", align_bytes=64)
            if by_vector > 0:
                nc.vector.tensor_copy(
                    out=grouped[:, :by_vector, :].rearrange("p (c i) j -> p c j i", i=4),
                    in_=source[:, :, :by_vector].rearrange("p j (c i) -> p c j i", i=4),
                )
            if by_vector < width:
                nc.scalar.activation(
                    grouped[:, by_vector:, :].rearrange("p (c i) j -> p c j i", i=4),
                    source[:, :, by_vector:].rearrange("p j (c i) -> p c j i", i=4),
                    ACT.Copy,
                )
            nc.vector.quantize_mx(
                out=x_codes[:, t0 : t0 + width].bitcast(FP8X4),
                scales=x_plane[:, t0 : t0 + width],
                in_=grouped[:].rearrange("p t j -> p (t j)"),
            )

        for i, (s0, width) in enumerate(zip(starts(SLOT_PIECES), SLOT_PIECES)):
            picks = offs_sb[:, s0 // 16 : (s0 + width) // 16]
            slot_codes = keep.tile([P, width], U32, name=f"slot_codes{i}", align_bytes=64)
            slot_plane = keep.tile([P, width], U8, name=f"slot_plane{i}", align_bytes=64)
            nc.vector.tensor_copy(slot_codes[:], x_codes[:].indirect(picks))
            nc.vector.tensor_copy(slot_plane[:], x_plane[:].indirect(picks))
            sums = psum.tile([P, width], F32, name=f"sums{i}", tag="work", bufs=5)
            for c0 in range(0, width, C):
                e = (s0 + c0) // C
                nc.tensor.matmul_mx(
                    out=sums[:, c0 : c0 + C],
                    lhsT=w_codes[:, e, :].bitcast(FP4X4),
                    lhsT_scale=w_plane[:, e, :],
                    rhs=slot_codes[:, c0 : c0 + C].bitcast(FP8X4),
                    rhs_scale=slot_plane[:, c0 : c0 + C],
                    start=True,
                    stop=True,
                )
            relu = keep.tile([P, width], F32, name=f"relu{i}")
            for c0 in range(0, width, C):
                e = (s0 + c0) // C
                nc.scalar.activation(relu[:, c0 : c0 + C], sums[:, c0 : c0 + C], ACT.Relu, bias=bias[:, e : e + 1])
            if i < SCALAR_SQUARES:
                nc.scalar.activation(y[:, s0 : s0 + width], relu[:], ACT.Square)
            else:
                nc.vector.tensor_tensor(y[:, s0 : s0 + width], relu[:], relu[:], ALU.mult)

        forth = [psum.tile([P, P], F32, name=f"forth{k}", tag="work", bufs=5) for k in range(turned // P)]

        def weigh(r, t0, width, gate_cols):
            weighted = keep.tile([P, width], F32, name=f"weighted{r}_{t0}")
            nc.vector.tensor_tensor(weighted[:], y[:].indirect(pos_sb[r][:, t0 // 16 : (t0 + width) // 16]), gate_cols, ALU.mult)
            return weighted

        def turn_and_add(r, weighted, t0, width):
            for c0 in range(0, width, P):
                nc.tensor.matmul(forth[(t0 + c0) // P][:], weighted[:, c0 : c0 + P], ident[:], start=(r == 0), stop=(r == TOP - 1), is_transpose=True)

        for r in range(TOP - 1):
            turn_and_add(r, weigh(r, 0, turned, gate_sb[r][:]), 0, turned)
        for i, (t0, width) in enumerate(zip(starts(TURNED_CHUNKS), TURNED_CHUNKS)):
            turn_and_add(TOP - 1, weigh(TOP - 1, t0, width, gate_sb[TOP - 1][:, t0 : t0 + width]), t0, width)
            back = psum.tile([P, width], F32, name=f"back{i}", tag="back", bufs=2)
            for c0 in range(0, width, P):
                summed = keep.tile([P, P], F32, name=f"summed{t0 + c0}")
                nc.scalar.activation(summed[:], forth[(t0 + c0) // P][:], ACT.Copy)
                nc.tensor.transpose(back[:, c0 : c0 + P], summed[:], ident[:])
            result = keep.tile([P, width], F32, name=f"result{i}")
            nc.scalar.activation(result[:], back[:], ACT.Copy)
            nc.sync.dma_start(out=out[:, t0 : t0 + width], in_=result[:])

        tail = [weigh(r, turned, T - turned, gate_tail[:, r, :]) for r in range(TOP - 1)]
        partial = keep.tile([P, 2, T - turned], F32, name="partial")
        nc.vector.tensor_tensor(partial[:, 0, :], tail[0][:], tail[1][:], ALU.add)
        tail.append(weigh(TOP - 1, turned, T - turned, gate_tail[:, TOP - 1, :]))
        nc.vector.tensor_tensor(partial[:, 1, :], partial[:, 0, :], tail[2][:], ALU.add)
        last = keep.tile([P, T - turned], F32, name="last")
        nc.vector.tensor_tensor(last[:], partial[:, 1, :], tail[3][:], ALU.add)
        nc.sync.dma_start(out=out[:, turned:], in_=last[:])
